import numpy as np
import ml_dtypes


def mxq(x, axis, fmt="e4m3"):
    dtype, down = {"e4m3": (ml_dtypes.float8_e4m3fn, 7), "e5m2": (ml_dtypes.float8_e5m2, 14)}[fmt]
    v = np.moveaxis(np.asarray(x, np.float32).astype(ml_dtypes.bfloat16).astype(np.float64), axis, -1)
    blocks = v.reshape(v.shape[:-1] + (-1, 32))
    amax = np.abs(blocks).max(-1, keepdims=True)
    byte = np.maximum(np.where(amax > 0, np.frexp(amax)[1] - 1 + 127, 0) - down, 1)
    scale = np.exp2(byte - 127.0)
    codes = (blocks / scale).astype(np.float32).astype(dtype).astype(np.float64)
    return np.moveaxis((codes * scale).reshape(v.shape), -1, axis)


WIDE = False


def mx_kscale(k):
    if not WIDE:
        return np.ones(k)
    levels = np.array([10, -10, 5, -5, 0])
    if k % 512:
        return np.exp2(np.random.permutation(np.resize(levels, k // 32))).repeat(32)
    a = np.empty((k // 512, 16))
    for p in range(k // 512):
        a[p, :8] = np.random.permutation(np.resize(levels, 8))
        for g in range(8):
            far = levels[np.abs(levels - a[p, g]) >= 10]
            a[p, g + 8] = far[np.random.randint(len(far))]
    return np.exp2(a.ravel()).repeat(32)


def f64(x):
    return np.asarray(x).astype(np.float64)


def striped(idx):
    return np.tile(idx.reshape(-1, 16).T, (8, 1)).astype(np.uint16)


def unstriped(offs):
    return offs[:16].T.reshape(-1).astype(np.int64)


E2M1 = np.array([0.0, 0.5, 1.0, 1.5, 2.0, 3.0, 4.0, 6.0, -0.0, -0.5, -1.0, -1.5, -2.0, -3.0, -4.0, -6.0])


def pack_weight(w, fmt):
    k, n = w.shape
    w = f64(np.asarray(w, np.float32).astype(ml_dtypes.bfloat16)).reshape(k // 32, 32, n)
    amax = np.abs(w).max(1)
    if fmt == "e4m3":
        byte = np.frexp(amax)[1] - 1 + 127 - 7
    else:
        mant, ex = np.frexp(amax / 6.0)
        byte = np.where(mant > 0.5, ex, ex - 1) + 127
    byte = np.clip(np.where(amax > 0, byte, 1), 1, 254)
    scaled = (w * np.exp2(127.0 - byte)[:, None, :]).reshape(k, n).astype(np.float32)
    by_word = np.ascontiguousarray(scaled.reshape(k // 512, 128, 4, n).transpose(0, 1, 3, 2))
    if fmt == "e4m3":
        words = by_word.astype(ml_dtypes.float8_e4m3fn).view(np.uint8)
    else:
        c = by_word.astype(ml_dtypes.float4_e2m1fn).view(np.uint8) & 0xF
        words = (c[..., 0::2] | (c[..., 1::2] << 4)).reshape(k // 512, 128, 2 * n)
    return np.ascontiguousarray(words), np.ascontiguousarray(byte.astype(np.uint8).reshape(k // 512, 16, n))


def unpack_weight(words, scales, fmt):
    g, _, n = scales.shape
    words = np.ascontiguousarray(words).reshape(g, 128, n, -1)
    if fmt == "e4m3":
        vals = words.view(ml_dtypes.float8_e4m3fn).astype(np.float64)
    else:
        nib = np.empty((g, 128, n, 4), np.uint8)
        nib[..., 0::2] = words & 0xF
        nib[..., 1::2] = words >> 4
        vals = E2M1[nib]
    vals = vals * np.repeat(np.exp2(scales.astype(np.float64) - 127.0), 8, axis=1)[..., None]
    return vals.transpose(0, 1, 3, 2).reshape(g * 512, n)


def gelu(v):
    return 0.5 * v * (1.0 + np.tanh(np.sqrt(2.0 / np.pi) * (v + 0.044715 * v**3)))


K, H, N, T, S, P, P2 = 512, 1024, 512, 4096, 1024, 512, 256

def setup_inputs():
    n = np.random.standard_normal
    s = mx_kscale(K)[:, None]
    u = mx_kscale(H)[:, None]
    gain = np.exp(0.3 * n((1, H))) * u.T
    d = {}
    d["tab_words"], d["tab_scales"] = pack_weight(n((K, T)) * s, "e4m3")
    d["offs"] = striped(np.random.permutation(T)[:S])
    d["pos1"] = striped(np.random.permutation(S)[:P])
    d["pos2"] = striped(np.random.permutation(P)[:P2])
    d["w1"] = (0.8 * n((K, H)) / K ** 0.5 / s * gain).astype(np.float32)
    d["w2"] = (3.0 * n((K, H)) / K ** 0.5 / s).astype(np.float32)
    d["w3_words"], d["w3_scales"] = pack_weight(1.5 * n((K, H)) / K ** 0.5 / s * gain, "e4m3")
    d["w4_words"], d["w4_scales"] = pack_weight(1.25 * n((H, H)) / H ** 0.5 / u, "e2m1")
    d["w5"] = (-1.25 * n((H, H)) / H ** 0.5 / u).astype(np.float32)
    d["w6"] = (1.3 * n((H, N)) / H ** 0.5 / u).astype(np.float32)
    return d

def reference(tab_words, tab_scales, offs, pos1, pos2, w1, w2, w3_words, w3_scales,
              w4_words, w4_scales, w5, w6):
    v = unpack_weight(tab_words, tab_scales, "e4m3")[:, unstriped(offs)]
    w3 = unpack_weight(w3_words, w3_scales, "e4m3")
    w4 = unpack_weight(w4_words, w4_scales, "e2m1")
    a = mxq(f64(w1), 0, "e4m3").T @ v
    b = mxq(f64(w2), 0, "e4m3").T @ v
    e = w3.T @ v
    h = a + e / (1.0 + np.exp(-b))
    x1 = h[:, unstriped(pos1)]
    x1q = mxq(x1, 0, "e4m3")
    y = w4.T @ x1q + mxq(f64(w5), 0, "e4m3").T @ x1q
    x2 = x1 + 0.9 * x1 * np.tanh(y)
    x3 = x2[:, unstriped(pos2)]
    o = mxq(f64(w6), 0, "e4m3").T @ mxq(x3, 0, "e4m3")
    return np.square(1.0 / (1.0 + np.exp(-o)))

@@ -1,0 +1,309 @@
+from contextlib import ExitStack
+
+import concourse.mybir as mybir
+
+F32 = mybir.dt.float32
+BF16 = mybir.dt.bfloat16
+I32 = mybir.dt.int32
+U32 = mybir.dt.uint32
+U16 = mybir.dt.uint16
+U8 = mybir.dt.uint8
+FP8X4 = mybir.dt.float8_e4m3fn_x4
+FP4X4 = mybir.dt.float4_e2m1fn_x4
+ACT = mybir.ActivationFunctionType
+ALU = mybir.AluOpType
+
+K, H, N, T, S, P1, P2 = 512, 1024, 512, 4096, 1024, 512, 256
+P = 128
+PACK = 4
+PASS = P * PACK
+BANK = 512
+POOL_ADDS = ()
+FLOPS = 2 * (3 * K * H * S + 2 * H * H * P1 + H * N * P2)
+
+
+def tile_list_postal_digit_doubt_kernel(
+    tc, tab_words, tab_scales, offs, pos1, pos2, w1, w2, w3_words, w3_scales, w4_words, w4_scales, w5, w6, out
+):
+    nc = tc.nc
+    with ExitStack() as ctx:
+        keep = ctx.enter_context(tc.tile_pool(name="keep", bufs=1))
+        ring = ctx.enter_context(tc.tile_pool(name="ring", bufs=2))
+        psum = ctx.enter_context(tc.psum_pool(name="psum", bufs=1))
+
+        def held(name, shape, dtype):
+            return keep.tile(shape, dtype, name=name, align_bytes=64)
+
+        tab_s = held("tab_s", [P, T], U8)
+        w3_s_raw = held("w3_s_raw", [P, H], U8)
+        w4_s_raw = held("w4_s_raw", [P, 2 * H], U8)
+        warm = held("warm", [P, 8], F32)
+        nc.vector.memset(tab_s[:].bitcast(I32), 0)
+        nc.vector.memset(warm[:, 0:1], 0.0)
+        nc.vector.memset(w3_s_raw[:].bitcast(I32), 0)
+        nc.vector.memset(w4_s_raw[:].bitcast(I32), 0)
+        nc.scalar.activation(warm[:, 4:5], warm[:, 0:1], ACT.Sigmoid)
+
+        offs_sb = keep.tile([P, S // 16], U16, name="offs_sb")
+        pos1_sb = keep.tile([P, P1 // 16], U16, name="pos1_sb")
+        pos2_sb = keep.tile([P, P2 // 16], U16, name="pos2_sb")
+        tab_w = held("tab_w", [P, T], I32)
+        w3_w_raw = held("w3_w_raw", [P, H], I32)
+        w4_w_raw = held("w4_w_raw", [P, 2, H // 2], I32)
+
+        def load_rows(name, w, a, c0):
+            raw = ring.tile([P, PACK, BANK], F32, name="raw", bufs=7)
+            nc.sync.dma_start(raw[:], w[PASS * a : PASS * (a + 1), c0 : c0 + BANK].rearrange("(p j) c -> p j c", j=PACK))
+            return raw
+
+        for q in range(4):
+            nc.sync.dma_start(tab_s[32 * q : 32 * q + 4, :].bitcast(I32), tab_scales[0, 4 * q : 4 * q + 4, :].bitcast(I32))
+        nc.sync.dma_start(offs_sb[:], offs)
+        nc.sync.dma_start(tab_w[:], tab_words[0].rearrange("p c i -> p (c i)").bitcast(I32))
+        raw2 = [load_rows("raw2_0", w2, 0, 0)]
+        w3_dram = w3_words[0].rearrange("p c i -> p (c i)").bitcast(I32)
+        nc.sync.dma_start(w3_w_raw[:, :BANK], w3_dram[:, :BANK])
+        for q in range(4):
+            nc.sync.dma_start(w3_s_raw[32 * q : 32 * q + 4, :].bitcast(I32), w3_scales[0, 4 * q : 4 * q + 4, :].bitcast(I32))
+        raw1 = [load_rows("raw1_0", w1, 0, 0)]
+        nc.sync.dma_start(pos1_sb[:], pos1)
+        raw2.append(load_rows("raw2_1", w2, 0, BANK))
+        nc.sync.dma_start(w3_w_raw[:, BANK:], w3_dram[:, BANK:])
+        raw1.append(load_rows("raw1_1", w1, 0, BANK))
+        for q in range(4):
+            nc.sync.dma_start(
+                w4_s_raw[32 * q : 32 * q + 4, :].bitcast(I32).rearrange("r (a c) -> r a c", a=2),
+                w4_scales[:, 4 * q : 4 * q + 4, :].bitcast(I32).rearrange("a r c -> r a c"),
+            )
+        nc.sync.dma_start(w4_w_raw[:], w4_words.bitcast(I32).rearrange("a p c -> p a c"))
+        raw5 = {}
+        for g in range(2):
+            for a in range(2):
+                raw5[a, g] = load_rows("raw5_%d%d" % (a, g), w5, a, BANK * g)
+        nc.sync.dma_start(pos2_sb[:], pos2)
+        raw6 = [load_rows("raw6_%d" % a, w6, a, 0) for a in range(2)]
+
+        def copy_on(engine, dst, src):
+            if engine == "s":
+                nc.scalar.copy(dst, src)
+            elif engine == "v":
+                nc.vector.tensor_copy(dst, src)
+            else:
+                nc.gpsimd.tensor_scalar(dst, src, 1.0, 0.0, ALU.mult, ALU.add)
+
+        def round_dealt(raw, engine, pieces):
+            grouped = ring.tile([P, PACK * BANK], BF16, name="grouped", bufs=3, align_bytes=64)
+            dst = grouped[:].rearrange("p (t m j) -> p m j t", t=PACK, j=PACK)
+            src = raw[:].rearrange("p j (m t) -> p m j t", t=PACK)
+            n = P // pieces
+            if engine == "sv":
+                copy_on("s", dst[:, :44], src[:, :44])
+                copy_on("v", dst[:, 44:], src[:, 44:])
+                return grouped
+            for i in range(pieces):
+                copy_on(engine, dst[:, n * i : n * (i + 1)], src[:, n * i : n * (i + 1)])
+            return grouped
+
+        def weave_views(grouped, planes):
+            dst = grouped[:].rearrange("p (c i t) -> p c t i", i=4, t=PACK)
+            src = planes[:].rearrange("p t (c i) -> p c t i", i=4)
+            return dst, src
+
+        def round_plain(raw, engine, pieces):
+            grouped = ring.tile([P, PACK * BANK], BF16, name="grouped", bufs=3, align_bytes=64)
+            dst, src = weave_views(grouped, raw)
+            n = P // pieces
+            for i in range(pieces):
+                copy_on(engine, dst[:, n * i : n * (i + 1)], src[:, n * i : n * (i + 1)])
+            return grouped
+
+        def quantise(name, grouped, width):
+            codes = held(name + "_codes", [P, width], U32)
+            scales = held(name + "_scales", [P, width], U8)
+            nc.vector.quantize_mx(out=codes[:].bitcast(FP8X4), scales=scales[:], in_=grouped[:])
+            return codes, scales
+
+        def mx(acc, lhs, col, rhs, start, stop):
+            nc.tensor.matmul_mx(
+                out=acc,
+                lhsT=lhs[0][:, col : col + P].bitcast(FP8X4),
+                lhsT_scale=lhs[1][:, col : col + P],
+                rhs=rhs[0][:].bitcast(FP8X4),
+                rhs_scale=rhs[1],
+                start=start,
+                stop=stop,
+            )
+
+        v_s = held("v_s", [P, S], U8)
+        nc.vector.tensor_copy(v_s[:], tab_s[:].indirect(offs_sb[:]))
+        v = []
+        for hf in range(2):
+            words = held("v_w%d" % hf, [P, BANK], U32)
+            cols = BANK // 16
+            nc.vector.tensor_copy(words[:], tab_w[:].bitcast(U32).indirect(offs_sb[:, cols * hf : cols * (hf + 1)]))
+            v.append((words, v_s[:, BANK * hf : BANK * (hf + 1)]))
+        w3_w = held("w3_w", [P, H], I32)
+        w3_s = held("w3_s", [P, H], U8)
+        nc.vector.tensor_copy(
+            w3_s[:].rearrange("p (g t m) -> p g m t", g=2, t=PACK), w3_s_raw[:].rearrange("p (g m t) -> p g m t", g=2, t=PACK)
+        )
+
+        def deal_w3(g):
+            cols = slice(BANK * g, BANK * (g + 1))
+            nc.vector.tensor_copy(
+                w3_w[:, cols].rearrange("p (t m) -> p m t", t=PACK), w3_w_raw[:, cols].rearrange("p (m t) -> p m t", t=PACK)
+            )
+
+        q2 = [quantise("q2_0", round_dealt(raw2[0], "sv", 2), BANK)]
+        deal_w3(0)
+        q1 = [quantise("q1_0", round_dealt(raw1[0], "s", 2), BANK)]
+
+        w4_w = held("w4_w", [P, 2, 2 * H], U8)
+        w4_s = held("w4_s", [P, 2 * H], U8)
+
+        def deal_w4():
+            for a in range(2):
+                nc.vector.tensor_copy(
+                    w4_w[:, a, :].bitcast(U16).rearrange("p (g t m) -> p g m t", g=2, t=PACK),
+                    w4_w_raw[:, a, :].bitcast(U16).rearrange("p (g m t) -> p g m t", g=2, t=PACK),
+                )
+            nc.vector.tensor_copy(
+                w4_s[:].rearrange("p (g t m) -> p g m t", g=4, t=PACK), w4_s_raw[:].rearrange("p (g m t) -> p g m t", g=4, t=PACK)
+            )
+
+        x1 = [held("x1_%d" % g, [P, PACK, P1], F32) for g in range(2)]
+        x3 = [held("x3_%d" % g, [P, PACK, P2], F32) for g in range(2)]
+        gated = {}
+        h = {}
+
+        def gate(g, t, hf):
+            b = psum.tile([P, BANK], F32, name="work", bufs=6)
+            mx(b[:], q2[g], P * t, v[hf], True, True)
+            e = psum.tile([P, BANK], F32, name="work", bufs=6)
+            mx(e[:], (w3_w, w3_s), BANK * g + P * t, v[hf], True, True)
+            sig = ring.tile([P, BANK], F32, name="sig", bufs=3)
+            nc.scalar.activation(sig[:], b[:], ACT.Sigmoid)
+            prod = ring.tile([P, BANK], F32, name="prod", bufs=8)
+            nc.vector.tensor_tensor(prod[:], e[:], sig[:], ALU.mult)
+            gated[g, t, hf] = prod
+
+        def add(g, t, hf):
+            if hf == 0:
+                h[g, t] = ring.tile([P, S], F32, name="h", bufs=3)
+            a = psum.tile([P, BANK], F32, name="work", bufs=6)
+            mx(a[:], q1[g], P * t, v[hf], True, True)
+            dst = h[g, t][:, BANK * hf : BANK * (hf + 1)]
+            if (g, t, hf) in POOL_ADDS:
+                a_sb = ring.tile([P, BANK], F32, name="a_sb", bufs=3)
+                nc.scalar.copy(a_sb[:], a[:])
+                nc.gpsimd.tensor_tensor(dst, a_sb[:], gated[g, t, hf][:], ALU.add)
+            else:
+                nc.vector.tensor_tensor(dst, a[:], gated[g, t, hf][:], ALU.add)
+
+        def pick1(g, t):
+            nc.vector.tensor_copy(x1[g][:, t, :], h[g, t][:].indirect(pos1_sb[:]))
+
+        def weave_x1(g, split):
+            grouped = ring.tile([P, PACK * P1], BF16, name="grouped", bufs=3, align_bytes=64)
+            dst, src = weave_views(grouped, x1[g])
+            if split > 0:
+                nc.vector.tensor_copy(dst[:, :split], src[:, :split])
+            nc.scalar.copy(dst[:, split:], src[:, split:])
+            return grouped
+
+        q5 = {}
+        q6 = []
+        x1q = []
+        y = {}
+
+        def y_passes(g, t, a):
+            if a == 0:
+                if 2 <= PACK * g + t < 6:
+                    y[g, t] = psum.tile([P, P1], F32, name="work", bufs=6)
+                else:
+                    y[g, t] = psum.tile([P, P1], F32, name="y", bufs=2)
+            col = BANK * g + P * t
+            nc.tensor.matmul_mx(
+                out=y[g, t][:],
+                lhsT=w4_w[:, a, 2 * col : 2 * (col + P)].bitcast(FP4X4),
+                lhsT_scale=w4_s[:, H * a + col : H * a + col + P],
+                rhs=x1q[a][0][:].bitcast(FP8X4),
+                rhs_scale=x1q[a][1][:],
+                start=(a == 0),
+                stop=False,
+            )
+            mx(y[g, t][:], q5[a, g], P * t, (x1q[a][0], x1q[a][1][:]), False, a == 1)
+
+        units = [(g, t, hf) for g in range(2) for t in range(PACK) for hf in range(2)]
+        extras = {
+            2: lambda: q2.append(quantise("q2_1", round_dealt(raw2[1], "s", 2), BANK)),
+            4: lambda: q1.append(quantise("q1_1", round_dealt(raw1[1], "s", 2), BANK)),
+            5: lambda: deal_w3(1),
+            6: deal_w4,
+            7: lambda: q5.setdefault((0, 0), quantise("q5_00", round_dealt(raw5[0, 0], "s", 2), BANK)),
+            9: lambda: q5.setdefault((1, 0), quantise("q5_10", round_dealt(raw5[1, 0], "s", 2), BANK)),
+            10: lambda: x1q.append(quantise("x1q_0", weave_x1(0, 0), P1)),
+            12: lambda: q5.setdefault((0, 1), quantise("q5_01", round_dealt(raw5[0, 1], "s", 2), BANK)),
+            14: lambda: q5.setdefault((1, 1), quantise("q5_11", round_dealt(raw5[1, 1], "s", 2), BANK)),
+        }
+        for i in range(len(units) + 2):
+            if i < len(units):
+                gate(*units[i])
+            if 1 <= i <= len(units):
+                add(*units[i - 1])
+            if i >= 2 and units[i - 2][2] == 1:
+                pick1(*units[i - 2][:2])
+            if i in extras:
+                extras[i]()
+        for i in range(6):
+            y_passes(i // PACK, i % PACK, 0)
+        x1q.append(quantise("x1q_1", weave_x1(1, 88), P1))
+        for a in range(2):
+            q6.append(quantise("q6_%d" % a, round_plain(raw6[a], "s", 2), N))
+
+        x2 = {}
+        x3q = []
+        o = []
+
+        def step(g, t):
+            if (g, t) not in y:
+                y_passes(g, t, 0)
+            y_passes(g, t, 1)
+            sig = ring.tile([P, P1], F32, name="sig", bufs=3)
+            nc.scalar.activation(sig[:], y[g, t][:], ACT.Sigmoid, scale=2.0)
+            x2[g, t] = ring.tile([P, P1], F32, name="x2", bufs=3)
+            nc.vector.scalar_tensor_tensor(x2[g, t][:], sig[:], 1.0 / 18.0, x1[g][:, t, :], ALU.add, ALU.mult)
+
+        def pick2(g, t):
+            nc.vector.tensor_copy(x3[g][:, t, :], x2[g, t][:].indirect(pos2_sb[:]))
+
+        def last_passes(g):
+            grouped = ring.tile([P, PACK * P2], BF16, name="x3_bf", bufs=2, align_bytes=64)
+            dst, src = weave_views(grouped, x3[g])
+            if g == 0:
+                nc.scalar.activation(dst, src, ACT.Copy, scale=1.8)
+            else:
+                nc.vector.tensor_scalar(dst, src, 1.8, None, ALU.mult)
+            codes, scales = quantise("x3q_%d" % g, grouped, P2)
+            for u in range(N // P):
+                if g == 0:
+                    o.append(psum.tile([P, P2], F32, name="work", bufs=6))
+                mx(o[u][:], q6[g], P * u, (codes, scales[:]), g == 0, g == 1)
+
+        tiles = [(g, t) for g in range(2) for t in range(PACK)]
+        for i in range(len(tiles) + 1):
+            if i < len(tiles):
+                step(*tiles[i])
+            if i >= 1:
+                pick2(*tiles[i - 1])
+            if i == PACK + 1:
+                last_passes(0)
+        last_passes(1)
+
+        for pair in range(2):
+            res = ring.tile([P, 2, P2], F32, name="res", bufs=2)
+            for k in range(2):
+                sig = ring.tile([P, P2], F32, name="sig_out", bufs=4)
+                nc.scalar.activation(sig[:], o[2 * pair + k][:], ACT.Sigmoid)
+                nc.vector.tensor_tensor(res[:, k, :], sig[:], sig[:], ALU.mult)
+            nc.sync.dma_start(out[2 * P * pair : 2 * P * (pair + 1), :].rearrange("(u p) j -> p u j", p=P), res[:])

@@ -18,7 +18,7 @@ P = 128
 PACK = 4
 PASS = P * PACK
 BANK = 512
-POOL_ADDS = ()
+POOL_ADDS = tuple((g, t, 0) for g in range(2) for t in range(4))
 FLOPS = 2 * (3 * K * H * S + 2 * H * H * P1 + H * N * P2)
 
 
@@ -48,7 +48,7 @@ def tile_list_postal_digit_doubt_kernel(
         pos1_sb = keep.tile([P, P1 // 16], U16, name="pos1_sb")
         pos2_sb = keep.tile([P, P2 // 16], U16, name="pos2_sb")
         tab_w = held("tab_w", [P, T], I32)
-        w3_w_raw = held("w3_w_raw", [P, H], I32)
+        w3_w_raw = [held("w3_w_raw%d" % g, [P, BANK], I32) for g in range(2)]
         w4_w_raw = held("w4_w_raw", [P, 2, H // 2], I32)
 
         def load_rows(name, w, a, c0):
@@ -56,27 +56,27 @@ def tile_list_postal_digit_doubt_kernel(
             nc.sync.dma_start(raw[:], w[PASS * a : PASS * (a + 1), c0 : c0 + BANK].rearrange("(p j) c -> p j c", j=PACK))
             return raw
 
+        raw1, raw2, raw5 = {}, {}, {}
+        w3_dram = w3_words[0].rearrange("p c i -> p (c i)").bitcast(I32)
+        nc.sync.dma_start(offs_sb[:], offs)
+        raw2[0] = load_rows("raw2_0", w2, 0, 0)
         for q in range(4):
             nc.sync.dma_start(tab_s[32 * q : 32 * q + 4, :].bitcast(I32), tab_scales[0, 4 * q : 4 * q + 4, :].bitcast(I32))
-        nc.sync.dma_start(offs_sb[:], offs)
         nc.sync.dma_start(tab_w[:], tab_words[0].rearrange("p c i -> p (c i)").bitcast(I32))
-        raw2 = [load_rows("raw2_0", w2, 0, 0)]
-        w3_dram = w3_words[0].rearrange("p c i -> p (c i)").bitcast(I32)
-        nc.sync.dma_start(w3_w_raw[:, :BANK], w3_dram[:, :BANK])
         for q in range(4):
             nc.sync.dma_start(w3_s_raw[32 * q : 32 * q + 4, :].bitcast(I32), w3_scales[0, 4 * q : 4 * q + 4, :].bitcast(I32))
-        raw1 = [load_rows("raw1_0", w1, 0, 0)]
+        nc.sync.dma_start(w3_w_raw[0][:], w3_dram[:, :BANK])
+        raw1[0] = load_rows("raw1_0", w1, 0, 0)
         nc.sync.dma_start(pos1_sb[:], pos1)
-        raw2.append(load_rows("raw2_1", w2, 0, BANK))
-        nc.sync.dma_start(w3_w_raw[:, BANK:], w3_dram[:, BANK:])
-        raw1.append(load_rows("raw1_1", w1, 0, BANK))
+        raw2[1] = load_rows("raw2_1", w2, 0, BANK)
+        nc.sync.dma_start(w3_w_raw[1][:], w3_dram[:, BANK:])
+        raw1[1] = load_rows("raw1_1", w1, 0, BANK)
         for q in range(4):
             nc.sync.dma_start(
                 w4_s_raw[32 * q : 32 * q + 4, :].bitcast(I32).rearrange("r (a c) -> r a c", a=2),
                 w4_scales[:, 4 * q : 4 * q + 4, :].bitcast(I32).rearrange("a r c -> r a c"),
             )
         nc.sync.dma_start(w4_w_raw[:], w4_words.bitcast(I32).rearrange("a p c -> p a c"))
-        raw5 = {}
         for g in range(2):
             for a in range(2):
                 raw5[a, g] = load_rows("raw5_%d%d" % (a, g), w5, a, BANK * g)
@@ -136,6 +136,7 @@ def tile_list_postal_digit_doubt_kernel(
 
         v_s = held("v_s", [P, S], U8)
         nc.vector.tensor_copy(v_s[:], tab_s[:].indirect(offs_sb[:]))
+        q2 = [quantise("q2_0", round_dealt(raw2[0], "s", 1), BANK)]
         v = []
         for hf in range(2):
             words = held("v_w%d" % hf, [P, BANK], U32)
@@ -151,12 +152,11 @@ def tile_list_postal_digit_doubt_kernel(
         def deal_w3(g):
             cols = slice(BANK * g, BANK * (g + 1))
             nc.vector.tensor_copy(
-                w3_w[:, cols].rearrange("p (t m) -> p m t", t=PACK), w3_w_raw[:, cols].rearrange("p (m t) -> p m t", t=PACK)
+                w3_w[:, cols].rearrange("p (t m) -> p m t", t=PACK), w3_w_raw[g][:].rearrange("p (m t) -> p m t", t=PACK)
             )
 
-        q2 = [quantise("q2_0", round_dealt(raw2[0], "sv", 2), BANK)]
         deal_w3(0)
-        q1 = [quantise("q1_0", round_dealt(raw1[0], "s", 2), BANK)]
+        q1 = [quantise("q1_0", round_dealt(raw1[0], "v", 1), BANK)]
 
         w4_w = held("w4_w", [P, 2, 2 * H], U8)
         w4_s = held("w4_s", [P, 2 * H], U8)

@@ -18,8 +18,9 @@ P = 128
 PACK = 4
 PASS = P * PACK
 BANK = 512
-POOL_ADDS = tuple((g, t, 0) for g in range(2) for t in range(4))
 FLOPS = 2 * (3 * K * H * S + 2 * H * H * P1 + H * N * P2)
+WEAVE_SPLIT = 88
+WEAVE3_SPLIT = 44
 
 
 def tile_list_postal_digit_doubt_kernel(
@@ -35,13 +36,15 @@ def tile_list_postal_digit_doubt_kernel(
             return keep.tile(shape, dtype, name=name, align_bytes=64)
 
         tab_s = held("tab_s", [P, T], U8)
-        w3_s_raw = held("w3_s_raw", [P, H], U8)
-        w4_s_raw = held("w4_s_raw", [P, 2 * H], U8)
+        w3_s_raw = held("w3_s_raw", [P, BANK], U8)
+        w4_s_raw = held("w4_s_raw", [P, H], U8)
+        w4_s = held("w4_s", [P, 2 * H], U8)
         warm = held("warm", [P, 8], F32)
         nc.vector.memset(tab_s[:].bitcast(I32), 0)
         nc.vector.memset(warm[:, 0:1], 0.0)
         nc.vector.memset(w3_s_raw[:].bitcast(I32), 0)
         nc.vector.memset(w4_s_raw[:].bitcast(I32), 0)
+        nc.vector.memset(w4_s[:, H:].bitcast(I32), 0)
         nc.scalar.activation(warm[:, 4:5], warm[:, 0:1], ACT.Sigmoid)
 
         offs_sb = keep.tile([P, S // 16], U16, name="offs_sb")
@@ -50,72 +53,48 @@ def tile_list_postal_digit_doubt_kernel(
         tab_w = held("tab_w", [P, T], I32)
         w3_w_raw = [held("w3_w_raw%d" % g, [P, BANK], I32) for g in range(2)]
         w4_w_raw = held("w4_w_raw", [P, 2, H // 2], I32)
+        w3_dram = w3_words[0].rearrange("p c i -> p (c i)").bitcast(I32)
 
-        def load_rows(name, w, a, c0):
-            raw = ring.tile([P, PACK, BANK], F32, name="raw", bufs=7)
+        def load_rows(w, a, c0):
+            raw = ring.tile([P, PACK, BANK], F32, name="raw", bufs=6)
             nc.sync.dma_start(raw[:], w[PASS * a : PASS * (a + 1), c0 : c0 + BANK].rearrange("(p j) c -> p j c", j=PACK))
             return raw
 
+        def load_scale_rows(tile, planes):
+            for q in range(4):
+                nc.sync.dma_start(
+                    tile[32 * q : 32 * q + 4 * planes.shape[0], :].bitcast(I32), planes[:, 4 * q : 4 * q + 4, :].bitcast(I32)
+                )
+
         raw1, raw2, raw5 = {}, {}, {}
-        w3_dram = w3_words[0].rearrange("p c i -> p (c i)").bitcast(I32)
         nc.sync.dma_start(offs_sb[:], offs)
-        raw2[0] = load_rows("raw2_0", w2, 0, 0)
-        for q in range(4):
-            nc.sync.dma_start(tab_s[32 * q : 32 * q + 4, :].bitcast(I32), tab_scales[0, 4 * q : 4 * q + 4, :].bitcast(I32))
-        nc.sync.dma_start(tab_w[:], tab_words[0].rearrange("p c i -> p (c i)").bitcast(I32))
-        for q in range(4):
-            nc.sync.dma_start(w3_s_raw[32 * q : 32 * q + 4, :].bitcast(I32), w3_scales[0, 4 * q : 4 * q + 4, :].bitcast(I32))
+        raw2[0] = load_rows(w2, 0, 0)
         nc.sync.dma_start(w3_w_raw[0][:], w3_dram[:, :BANK])
-        raw1[0] = load_rows("raw1_0", w1, 0, 0)
+        load_scale_rows(tab_s, tab_scales)
+        nc.sync.dma_start(tab_w[:], tab_words[0].rearrange("p c i -> p (c i)").bitcast(I32))
+        load_scale_rows(w3_s_raw, w3_scales[0].rearrange("q (g c) -> g q c", g=2))
+        raw1[0] = load_rows(w1, 0, 0)
         nc.sync.dma_start(pos1_sb[:], pos1)
-        raw2[1] = load_rows("raw2_1", w2, 0, BANK)
-        nc.sync.dma_start(w3_w_raw[1][:], w3_dram[:, BANK:])
-        raw1[1] = load_rows("raw1_1", w1, 0, BANK)
-        for q in range(4):
-            nc.sync.dma_start(
-                w4_s_raw[32 * q : 32 * q + 4, :].bitcast(I32).rearrange("r (a c) -> r a c", a=2),
-                w4_scales[:, 4 * q : 4 * q + 4, :].bitcast(I32).rearrange("a r c -> r a c"),
-            )
         nc.sync.dma_start(w4_w_raw[:], w4_words.bitcast(I32).rearrange("a p c -> p a c"))
+        raw2[1] = load_rows(w2, 0, BANK)
+        nc.sync.dma_start(w3_w_raw[1][:], w3_dram[:, BANK:])
+        raw1[1] = load_rows(w1, 0, BANK)
         for g in range(2):
             for a in range(2):
-                raw5[a, g] = load_rows("raw5_%d%d" % (a, g), w5, a, BANK * g)
+                raw5[a, g] = load_rows(w5, a, BANK * g)
         nc.sync.dma_start(pos2_sb[:], pos2)
-        raw6 = [load_rows("raw6_%d" % a, w6, a, 0) for a in range(2)]
+        load_scale_rows(w4_s_raw, w4_scales)
+        raw6 = [load_rows(w6, a, 0) for a in range(2)]
 
-        def copy_on(engine, dst, src):
-            if engine == "s":
-                nc.scalar.copy(dst, src)
-            elif engine == "v":
-                nc.vector.tensor_copy(dst, src)
-            else:
-                nc.gpsimd.tensor_scalar(dst, src, 1.0, 0.0, ALU.mult, ALU.add)
-
-        def round_dealt(raw, engine, pieces):
-            grouped = ring.tile([P, PACK * BANK], BF16, name="grouped", bufs=3, align_bytes=64)
-            dst = grouped[:].rearrange("p (t m j) -> p m j t", t=PACK, j=PACK)
+        def dealt_views(grouped, raw):
+            dst = grouped.rearrange("p (t m j) -> p m j t", t=PACK, j=PACK)
             src = raw[:].rearrange("p j (m t) -> p m j t", t=PACK)
-            n = P // pieces
-            if engine == "sv":
-                copy_on("s", dst[:, :44], src[:, :44])
-                copy_on("v", dst[:, 44:], src[:, 44:])
-                return grouped
-            for i in range(pieces):
-                copy_on(engine, dst[:, n * i : n * (i + 1)], src[:, n * i : n * (i + 1)])
-            return grouped
-
-        def weave_views(grouped, planes):
-            dst = grouped[:].rearrange("p (c i t) -> p c t i", i=4, t=PACK)
-            src = planes[:].rearrange("p t (c i) -> p c t i", i=4)
             return dst, src
 
-        def round_plain(raw, engine, pieces):
-            grouped = ring.tile([P, PACK * BANK], BF16, name="grouped", bufs=3, align_bytes=64)
-            dst, src = weave_views(grouped, raw)
-            n = P // pieces
-            for i in range(pieces):
-                copy_on(engine, dst[:, n * i : n * (i + 1)], src[:, n * i : n * (i + 1)])
-            return grouped
+        def woven_views(grouped, planes):
+            dst = grouped.rearrange("p (c i t) -> p c t i", i=4, t=PACK)
+            src = planes[:].rearrange("p t (c i) -> p c t i", i=4)
+            return dst, src
 
         def quantise(name, grouped, width):
             codes = held(name + "_codes", [P, width], U32)
@@ -123,12 +102,23 @@ def tile_list_postal_digit_doubt_kernel(
             nc.vector.quantize_mx(out=codes[:].bitcast(FP8X4), scales=scales[:], in_=grouped[:])
             return codes, scales
 
+        def quantise_weights(name, raws, views):
+            width = PACK * BANK
+            grouped = ring.tile([P, width * len(raws)], BF16, name="grouped%d" % len(raws), bufs=2, align_bytes=64)
+            for i, raw in enumerate(raws):
+                dst, src = views(grouped[:, width * i : width * (i + 1)], raw)
+                for half in range(2):
+                    rows = slice(P // 2 * half, P // 2 * (half + 1))
+                    nc.scalar.copy(dst[:, rows], src[:, rows])
+            codes, scales = quantise(name, grouped, BANK * len(raws))
+            return [(codes[:, BANK * i : BANK * (i + 1)], scales[:, BANK * i : BANK * (i + 1)]) for i in range(len(raws))]
+
         def mx(acc, lhs, col, rhs, start, stop):
             nc.tensor.matmul_mx(
                 out=acc,
                 lhsT=lhs[0][:, col : col + P].bitcast(FP8X4),
                 lhsT_scale=lhs[1][:, col : col + P],
-                rhs=rhs[0][:].bitcast(FP8X4),
+                rhs=rhs[0].bitcast(FP8X4),
                 rhs_scale=rhs[1],
                 start=start,
                 stop=stop,
@@ -136,40 +126,43 @@ def tile_list_postal_digit_doubt_kernel(
 
         v_s = held("v_s", [P, S], U8)
         nc.vector.tensor_copy(v_s[:], tab_s[:].indirect(offs_sb[:]))
-        q2 = [quantise("q2_0", round_dealt(raw2[0], "s", 1), BANK)]
+        q2 = quantise_weights("q2_0", [raw2[0]], dealt_views)
+        w3_w = held("w3_w", [P, H], I32)
+        w3_s = held("w3_s", [P, BANK], U8)
+        w4_w = held("w4_w", [P, 2, 2 * H], U8)
         v = []
-        for hf in range(2):
+
+        def gather_words(hf):
             words = held("v_w%d" % hf, [P, BANK], U32)
             cols = BANK // 16
             nc.vector.tensor_copy(words[:], tab_w[:].bitcast(U32).indirect(offs_sb[:, cols * hf : cols * (hf + 1)]))
-            v.append((words, v_s[:, BANK * hf : BANK * (hf + 1)]))
-        w3_w = held("w3_w", [P, H], I32)
-        w3_s = held("w3_s", [P, H], U8)
-        nc.vector.tensor_copy(
-            w3_s[:].rearrange("p (g t m) -> p g m t", g=2, t=PACK), w3_s_raw[:].rearrange("p (g m t) -> p g m t", g=2, t=PACK)
-        )
+            v.append((words[:], v_s[:, BANK * hf : BANK * (hf + 1)]))
 
-        def deal_w3(g):
-            cols = slice(BANK * g, BANK * (g + 1))
+        def deal(dst, src):
             nc.vector.tensor_copy(
-                w3_w[:, cols].rearrange("p (t m) -> p m t", t=PACK), w3_w_raw[g][:].rearrange("p (m t) -> p m t", t=PACK)
+                dst.rearrange("p (g t m) -> p g t m", t=PACK, m=P), src.rearrange("p (g m t) -> p g t m", t=PACK, m=P)
             )
 
-        deal_w3(0)
-        q1 = [quantise("q1_0", round_dealt(raw1[0], "v", 1), BANK)]
-
-        w4_w = held("w4_w", [P, 2, 2 * H], U8)
-        w4_s = held("w4_s", [P, 2 * H], U8)
+        def deal_w3_words(g):
+            nc.vector.tensor_copy(
+                w3_w[:, BANK * g : BANK * (g + 1)].rearrange("p (t m) -> p m t", t=PACK),
+                w3_w_raw[g][:].rearrange("p (m t) -> p m t", t=PACK),
+            )
 
         def deal_w4():
             for a in range(2):
-                nc.vector.tensor_copy(
-                    w4_w[:, a, :].bitcast(U16).rearrange("p (g t m) -> p g m t", g=2, t=PACK),
-                    w4_w_raw[:, a, :].bitcast(U16).rearrange("p (g m t) -> p g m t", g=2, t=PACK),
-                )
-            nc.vector.tensor_copy(
-                w4_s[:].rearrange("p (g t m) -> p g m t", g=4, t=PACK), w4_s_raw[:].rearrange("p (g m t) -> p g m t", g=4, t=PACK)
-            )
+                deal(w4_w[:, a, :].bitcast(U16), w4_w_raw[:, a, :].bitcast(U16))
+
+        def deal_w4_scales():
+            deal(w4_s[:, :H], w4_s_raw[:])
+            for q in range(4):
+                nc.sync.dma_start(w4_s[32 * q : 32 * q + 4, H:].bitcast(I32), w4_s[32 * q + 4 : 32 * q + 8, :H].bitcast(I32))
+
+        deal_w3_words(0)
+        gather_words(0)
+        deal(w3_s[:], w3_s_raw[:])
+        gather_words(1)
+        q1 = []
 
         x1 = [held("x1_%d" % g, [P, PACK, P1], F32) for g in range(2)]
         x3 = [held("x3_%d" % g, [P, PACK, P2], F32) for g in range(2)]
@@ -180,7 +173,7 @@ def tile_list_postal_digit_doubt_kernel(
             b = psum.tile([P, BANK], F32, name="work", bufs=6)
             mx(b[:], q2[g], P * t, v[hf], True, True)
             e = psum.tile([P, BANK], F32, name="work", bufs=6)
-            mx(e[:], (w3_w, w3_s), BANK * g + P * t, v[hf], True, True)
+            mx(e[:], (w3_w[:, BANK * g : BANK * (g + 1)], w3_s[4 * g :, :]), P * t, v[hf], True, True)
             sig = ring.tile([P, BANK], F32, name="sig", bufs=3)
             nc.scalar.activation(sig[:], b[:], ACT.Sigmoid)
             prod = ring.tile([P, BANK], F32, name="prod", bufs=8)
@@ -192,33 +185,35 @@ def tile_list_postal_digit_doubt_kernel(
                 h[g, t] = ring.tile([P, S], F32, name="h", bufs=3)
             a = psum.tile([P, BANK], F32, name="work", bufs=6)
             mx(a[:], q1[g], P * t, v[hf], True, True)
-            dst = h[g, t][:, BANK * hf : BANK * (hf + 1)]
-            if (g, t, hf) in POOL_ADDS:
-                a_sb = ring.tile([P, BANK], F32, name="a_sb", bufs=3)
-                nc.scalar.copy(a_sb[:], a[:])
-                nc.gpsimd.tensor_tensor(dst, a_sb[:], gated[g, t, hf][:], ALU.add)
-            else:
-                nc.vector.tensor_tensor(dst, a[:], gated[g, t, hf][:], ALU.add)
+            nc.vector.tensor_tensor(h[g, t][:, BANK * hf : BANK * (hf + 1)], a[:], gated[g, t, hf][:], ALU.add)
 
         def pick1(g, t):
             nc.vector.tensor_copy(x1[g][:, t, :], h[g, t][:].indirect(pos1_sb[:]))
 
-        def weave_x1(g, split):
-            grouped = ring.tile([P, PACK * P1], BF16, name="grouped", bufs=3, align_bytes=64)
-            dst, src = weave_views(grouped, x1[g])
-            if split > 0:
-                nc.vector.tensor_copy(dst[:, :split], src[:, :split])
-            nc.scalar.copy(dst[:, split:], src[:, split:])
-            return grouped
-
         q5 = {}
-        q6 = []
         x1q = []
         y = {}
 
+        def quantise_x1(g, split):
+            grouped = ring.tile([P, PACK * P1], BF16, name="grouped1", bufs=2, align_bytes=64)
+            dst, src = woven_views(grouped[:], x1[g])
+            if split > 0:
+                nc.vector.tensor_copy(dst[:, :split], src[:, :split])
+            nc.scalar.copy(dst[:, split:], src[:, split:])
+            codes, scales = quantise("x1q_%d" % g, grouped, P1)
+            x1q.append((codes[:], scales[:]))
+
+        def quantise_second_halves():
+            both = quantise_weights("q21_1", [raw2[1], raw1[1]], dealt_views)
+            q2.append(both[0])
+            q1.append(both[1])
+
+        def quantise_w5(g):
+            q5[g] = quantise_weights("q5_%d" % g, [raw5[0, g], raw5[1, g]], dealt_views)
+
         def y_passes(g, t, a):
             if a == 0:
-                if 2 <= PACK * g + t < 6:
+                if PACK * g + t >= 2:
                     y[g, t] = psum.tile([P, P1], F32, name="work", bufs=6)
                 else:
                     y[g, t] = psum.tile([P, P1], F32, name="y", bufs=2)
@@ -227,47 +222,44 @@ def tile_list_postal_digit_doubt_kernel(
                 out=y[g, t][:],
                 lhsT=w4_w[:, a, 2 * col : 2 * (col + P)].bitcast(FP4X4),
                 lhsT_scale=w4_s[:, H * a + col : H * a + col + P],
-                rhs=x1q[a][0][:].bitcast(FP8X4),
-                rhs_scale=x1q[a][1][:],
+                rhs=x1q[a][0].bitcast(FP8X4),
+                rhs_scale=x1q[a][1],
                 start=(a == 0),
                 stop=False,
             )
-            mx(y[g, t][:], q5[a, g], P * t, (x1q[a][0], x1q[a][1][:]), False, a == 1)
+            mx(y[g, t][:], q5[g][a], P * t, x1q[a], False, a == 1)
 
         units = [(g, t, hf) for g in range(2) for t in range(PACK) for hf in range(2)]
         extras = {
-            2: lambda: q2.append(quantise("q2_1", round_dealt(raw2[1], "s", 2), BANK)),
-            4: lambda: q1.append(quantise("q1_1", round_dealt(raw1[1], "s", 2), BANK)),
-            5: lambda: deal_w3(1),
+            0: lambda: q1.extend(quantise_weights("q1_0", [raw1[0]], dealt_views)),
+            3: quantise_second_halves,
+            5: lambda: deal_w3_words(1),
             6: deal_w4,
-            7: lambda: q5.setdefault((0, 0), quantise("q5_00", round_dealt(raw5[0, 0], "s", 2), BANK)),
-            9: lambda: q5.setdefault((1, 0), quantise("q5_10", round_dealt(raw5[1, 0], "s", 2), BANK)),
-            10: lambda: x1q.append(quantise("x1q_0", weave_x1(0, 0), P1)),
-            12: lambda: q5.setdefault((0, 1), quantise("q5_01", round_dealt(raw5[0, 1], "s", 2), BANK)),
-            14: lambda: q5.setdefault((1, 1), quantise("q5_11", round_dealt(raw5[1, 1], "s", 2), BANK)),
+            9: lambda: quantise_w5(0),
+            10: deal_w4_scales,
+            11: lambda: quantise_x1(0, 0),
+            13: lambda: quantise_w5(1),
         }
-        for i in range(len(units) + 2):
+        LAG = 1
+        for i in range(len(units) + LAG + 1):
             if i < len(units):
                 gate(*units[i])
-            if 1 <= i <= len(units):
-                add(*units[i - 1])
-            if i >= 2 and units[i - 2][2] == 1:
-                pick1(*units[i - 2][:2])
+            if LAG <= i < len(units) + LAG:
+                add(*units[i - LAG])
+            if i > LAG and units[i - LAG - 1][2] == 1:
+                pick1(*units[i - LAG - 1][:2])
             if i in extras:
                 extras[i]()
-        for i in range(6):
-            y_passes(i // PACK, i % PACK, 0)
-        x1q.append(quantise("x1q_1", weave_x1(1, 88), P1))
-        for a in range(2):
-            q6.append(quantise("q6_%d" % a, round_plain(raw6[a], "s", 2), N))
+        tiles = [(g, t) for g in range(2) for t in range(PACK)]
+        for g, t in tiles:
+            y_passes(g, t, 0)
+        quantise_x1(1, WEAVE_SPLIT)
+        q6 = quantise_weights("q6", raw6, woven_views)
 
         x2 = {}
-        x3q = []
         o = []
 
         def step(g, t):
-            if (g, t) not in y:
-                y_passes(g, t, 0)
             y_passes(g, t, 1)
             sig = ring.tile([P, P1], F32, name="sig", bufs=3)
             nc.scalar.activation(sig[:], y[g, t][:], ACT.Sigmoid, scale=2.0)
@@ -277,33 +269,30 @@ def tile_list_postal_digit_doubt_kernel(
         def pick2(g, t):
             nc.vector.tensor_copy(x3[g][:, t, :], x2[g, t][:].indirect(pos2_sb[:]))
 
-        def last_passes(g):
+        def last_passes(g, split):
             grouped = ring.tile([P, PACK * P2], BF16, name="x3_bf", bufs=2, align_bytes=64)
-            dst, src = weave_views(grouped, x3[g])
-            if g == 0:
-                nc.scalar.activation(dst, src, ACT.Copy, scale=1.8)
-            else:
-                nc.vector.tensor_scalar(dst, src, 1.8, None, ALU.mult)
+            dst, src = woven_views(grouped[:], x3[g])
+            if split > 0:
+                nc.vector.tensor_scalar(dst[:, :split], src[:, :split], 1.8, None, ALU.mult)
+            nc.scalar.activation(dst[:, split:], src[:, split:], ACT.Copy, scale=1.8)
             codes, scales = quantise("x3q_%d" % g, grouped, P2)
             for u in range(N // P):
                 if g == 0:
                     o.append(psum.tile([P, P2], F32, name="work", bufs=6))
-                mx(o[u][:], q6[g], P * u, (codes, scales[:]), g == 0, g == 1)
+                mx(o[u][:], q6[g], P * u, (codes[:], scales[:]), g == 0, g == 1)
 
-        tiles = [(g, t) for g in range(2) for t in range(PACK)]
         for i in range(len(tiles) + 1):
             if i < len(tiles):
                 step(*tiles[i])
             if i >= 1:
                 pick2(*tiles[i - 1])
             if i == PACK + 1:
-                last_passes(0)
-        last_passes(1)
+                last_passes(0, 0)
+        last_passes(1, WEAVE3_SPLIT)
 
-        for pair in range(2):
-            res = ring.tile([P, 2, P2], F32, name="res", bufs=2)
-            for k in range(2):
-                sig = ring.tile([P, P2], F32, name="sig_out", bufs=4)
-                nc.scalar.activation(sig[:], o[2 * pair + k][:], ACT.Sigmoid)
-                nc.vector.tensor_tensor(res[:, k, :], sig[:], sig[:], ALU.mult)
-            nc.sync.dma_start(out[2 * P * pair : 2 * P * (pair + 1), :].rearrange("(u p) j -> p u j", p=P), res[:])
+        for u in range(N // P):
+            sig = ring.tile([P, P2], F32, name="sig_out", bufs=4)
+            nc.scalar.activation(sig[:], o[u][:], ACT.Sigmoid)
+            res = ring.tile([P, P2], F32, name="res", bufs=4)
+            nc.vector.tensor_tensor(res[:], sig[:], sig[:], ALU.mult)
+            nc.sync.dma_start(out[P * u : P * (u + 1), :], res[:])

@@ -19,6 +19,7 @@ PACK = 4
 PASS = P * PACK
 BANK = 512
 FLOPS = 2 * (3 * K * H * S + 2 * H * H * P1 + H * N * P2)
+POOL_COLS = 384
 WEAVE_SPLIT = 88
 WEAVE3_SPLIT = 44
 
@@ -87,8 +88,8 @@ def tile_list_postal_digit_doubt_kernel(
         raw6 = [load_rows(w6, a, 0) for a in range(2)]
 
         def dealt_views(grouped, raw):
-            dst = grouped.rearrange("p (t m j) -> p m j t", t=PACK, j=PACK)
-            src = raw[:].rearrange("p j (m t) -> p m j t", t=PACK)
+            dst = grouped.rearrange("p (t n i j) -> p n j i t", t=PACK, i=2, j=PACK)
+            src = raw[:].rearrange("p j (n i t) -> p n j i t", i=2, t=PACK)
             return dst, src
 
         def woven_views(grouped, planes):
@@ -108,7 +109,7 @@ def tile_list_postal_digit_doubt_kernel(
             for i, raw in enumerate(raws):
                 dst, src = views(grouped[:, width * i : width * (i + 1)], raw)
                 for half in range(2):
-                    rows = slice(P // 2 * half, P // 2 * (half + 1))
+                    rows = slice(dst.shape[1] // 2 * half, dst.shape[1] // 2 * (half + 1))
                     nc.scalar.copy(dst[:, rows], src[:, rows])
             codes, scales = quantise(name, grouped, BANK * len(raws))
             return [(codes[:, BANK * i : BANK * (i + 1)], scales[:, BANK * i : BANK * (i + 1)]) for i in range(len(raws))]
@@ -185,7 +186,14 @@ def tile_list_postal_digit_doubt_kernel(
                 h[g, t] = ring.tile([P, S], F32, name="h", bufs=3)
             a = psum.tile([P, BANK], F32, name="work", bufs=6)
             mx(a[:], q1[g], P * t, v[hf], True, True)
-            nc.vector.tensor_tensor(h[g, t][:, BANK * hf : BANK * (hf + 1)], a[:], gated[g, t, hf][:], ALU.add)
+            dst, prod = h[g, t][:, BANK * hf : BANK * (hf + 1)], gated[g, t, hf]
+            first = POOL_COLS if hf == 0 else 0
+            if first:
+                a_sb = ring.tile([P, POOL_COLS], F32, name="a_sb", bufs=2)
+                nc.scalar.copy(a_sb[:], a[:, :first])
+                nc.gpsimd.tensor_tensor(dst[:, :first], a_sb[:], prod[:, :first], ALU.add)
+            if first < BANK:
+                nc.vector.tensor_tensor(dst[:, first:], a[:, first:], prod[:, first:], ALU.add)
 
         def pick1(g, t):
             nc.vector.tensor_copy(x1[g][:, t, :], h[g, t][:].indirect(pos1_sb[:]))

@@ -14,14 +14,25 @@ ACT = mybir.ActivationFunctionType
 ALU = mybir.AluOpType
 
 K, H, N, T, S, P1, P2 = 512, 1024, 512, 4096, 1024, 512, 256
+FLOPS = 2 * (3 * K * H * S + 2 * H * H * P1 + H * N * P2)
+
 P = 128
 PACK = 4
 PASS = P * PACK
 BANK = 512
-FLOPS = 2 * (3 * K * H * S + 2 * H * H * P1 + H * N * P2)
+QUADRANTS = 4
+STEP_GAIN = 1.8
+STEP_SHIFT = 1.0 / 18.0
+
 POOL_COLS = 384
-WEAVE_SPLIT = 88
-WEAVE3_SPLIT = 44
+X1_RUNS_ON_VECTOR = 88
+X3_RUNS_ON_VECTOR = 44
+
+RAW_BUFS = 6
+GATED_BUFS = 8
+STREAM_BUFS = 3
+WORK_BANKS = 6
+EARLY_BANKS = 2
 
 
 def tile_list_postal_digit_doubt_kernel(
@@ -40,13 +51,10 @@ def tile_list_postal_digit_doubt_kernel(
         w3_s_raw = held("w3_s_raw", [P, BANK], U8)
         w4_s_raw = held("w4_s_raw", [P, H], U8)
         w4_s = held("w4_s", [P, 2 * H], U8)
-        warm = held("warm", [P, 8], F32)
         nc.vector.memset(tab_s[:].bitcast(I32), 0)
-        nc.vector.memset(warm[:, 0:1], 0.0)
         nc.vector.memset(w3_s_raw[:].bitcast(I32), 0)
         nc.vector.memset(w4_s_raw[:].bitcast(I32), 0)
         nc.vector.memset(w4_s[:, H:].bitcast(I32), 0)
-        nc.scalar.activation(warm[:, 4:5], warm[:, 0:1], ACT.Sigmoid)
 
         offs_sb = keep.tile([P, S // 16], U16, name="offs_sb")
         pos1_sb = keep.tile([P, P1 // 16], U16, name="pos1_sb")
@@ -56,15 +64,17 @@ def tile_list_postal_digit_doubt_kernel(
         w4_w_raw = held("w4_w_raw", [P, 2, H // 2], I32)
         w3_dram = w3_words[0].rearrange("p c i -> p (c i)").bitcast(I32)
 
-        def load_rows(w, a, c0):
-            raw = ring.tile([P, PACK, BANK], F32, name="raw", bufs=6)
-            nc.sync.dma_start(raw[:], w[PASS * a : PASS * (a + 1), c0 : c0 + BANK].rearrange("(p j) c -> p j c", j=PACK))
+        def load_rows(w, a, g):
+            raw = ring.tile([P, PACK, BANK], F32, name="raw", bufs=RAW_BUFS)
+            piece = w[PASS * a : PASS * (a + 1), BANK * g : BANK * (g + 1)]
+            nc.sync.dma_start(raw[:], piece.rearrange("(p j) c -> p j c", j=PACK))
             return raw
 
-        def load_scale_rows(tile, planes):
-            for q in range(4):
+        def load_scale_rows(tile, row_sets):
+            for quad in range(QUADRANTS):
                 nc.sync.dma_start(
-                    tile[32 * q : 32 * q + 4 * planes.shape[0], :].bitcast(I32), planes[:, 4 * q : 4 * q + 4, :].bitcast(I32)
+                    tile[32 * quad : 32 * quad + 4 * row_sets.shape[0], :].bitcast(I32),
+                    row_sets[:, 4 * quad : 4 * quad + 4, :].bitcast(I32),
                 )
 
         raw1, raw2, raw5 = {}, {}, {}
@@ -77,41 +87,41 @@ def tile_list_postal_digit_doubt_kernel(
         raw1[0] = load_rows(w1, 0, 0)
         nc.sync.dma_start(pos1_sb[:], pos1)
         nc.sync.dma_start(w4_w_raw[:], w4_words.bitcast(I32).rearrange("a p c -> p a c"))
-        raw2[1] = load_rows(w2, 0, BANK)
+        raw2[1] = load_rows(w2, 0, 1)
         nc.sync.dma_start(w3_w_raw[1][:], w3_dram[:, BANK:])
-        raw1[1] = load_rows(w1, 0, BANK)
+        raw1[1] = load_rows(w1, 0, 1)
         for g in range(2):
             for a in range(2):
-                raw5[a, g] = load_rows(w5, a, BANK * g)
+                raw5[a, g] = load_rows(w5, a, g)
         nc.sync.dma_start(pos2_sb[:], pos2)
         load_scale_rows(w4_s_raw, w4_scales)
         raw6 = [load_rows(w6, a, 0) for a in range(2)]
 
-        def dealt_views(grouped, raw):
-            dst = grouped.rearrange("p (t n i j) -> p n j i t", t=PACK, i=2, j=PACK)
+        def dealt_views(rounded, raw):
+            dst = rounded.rearrange("p (t n i j) -> p n j i t", t=PACK, i=2, j=PACK)
             src = raw[:].rearrange("p j (n i t) -> p n j i t", i=2, t=PACK)
             return dst, src
 
-        def woven_views(grouped, planes):
-            dst = grouped.rearrange("p (c i t) -> p c t i", i=4, t=PACK)
-            src = planes[:].rearrange("p t (c i) -> p c t i", i=4)
+        def woven_views(rounded, rows):
+            dst = rounded.rearrange("p (c i t) -> p c t i", i=4, t=PACK)
+            src = rows[:].rearrange("p t (c i) -> p c t i", i=4)
             return dst, src
 
-        def quantise(name, grouped, width):
+        def quantise(name, rounded, width):
             codes = held(name + "_codes", [P, width], U32)
             scales = held(name + "_scales", [P, width], U8)
-            nc.vector.quantize_mx(out=codes[:].bitcast(FP8X4), scales=scales[:], in_=grouped[:])
+            nc.vector.quantize_mx(out=codes[:].bitcast(FP8X4), scales=scales[:], in_=rounded[:])
             return codes, scales
 
         def quantise_weights(name, raws, views):
             width = PACK * BANK
-            grouped = ring.tile([P, width * len(raws)], BF16, name="grouped%d" % len(raws), bufs=2, align_bytes=64)
+            rounded = ring.tile([P, width * len(raws)], BF16, name="grouped%d" % len(raws), bufs=2, align_bytes=64)
             for i, raw in enumerate(raws):
-                dst, src = views(grouped[:, width * i : width * (i + 1)], raw)
-                for half in range(2):
-                    rows = slice(dst.shape[1] // 2 * half, dst.shape[1] // 2 * (half + 1))
-                    nc.scalar.copy(dst[:, rows], src[:, rows])
-            codes, scales = quantise(name, grouped, BANK * len(raws))
+                dst, src = views(rounded[:, width * i : width * (i + 1)], raw)
+                for part in range(2):
+                    runs = slice(dst.shape[1] // 2 * part, dst.shape[1] // 2 * (part + 1))
+                    nc.scalar.copy(dst[:, runs], src[:, runs])
+            codes, scales = quantise(name, rounded, BANK * len(raws))
             return [(codes[:, BANK * i : BANK * (i + 1)], scales[:, BANK * i : BANK * (i + 1)]) for i in range(len(raws))]
 
         def mx(acc, lhs, col, rhs, start, stop):
@@ -133,11 +143,11 @@ def tile_list_postal_digit_doubt_kernel(
         w4_w = held("w4_w", [P, 2, 2 * H], U8)
         v = []
 
-        def gather_words(hf):
-            words = held("v_w%d" % hf, [P, BANK], U32)
+        def gather_words(half):
+            words = held("v_w%d" % half, [P, BANK], U32)
             cols = BANK // 16
-            nc.vector.tensor_copy(words[:], tab_w[:].bitcast(U32).indirect(offs_sb[:, cols * hf : cols * (hf + 1)]))
-            v.append((words[:], v_s[:, BANK * hf : BANK * (hf + 1)]))
+            nc.vector.tensor_copy(words[:], tab_w[:].bitcast(U32).indirect(offs_sb[:, cols * half : cols * (half + 1)]))
+            v.append((words[:], v_s[:, BANK * half : BANK * (half + 1)]))
 
         def deal(dst, src):
             nc.vector.tensor_copy(
@@ -150,14 +160,15 @@ def tile_list_postal_digit_doubt_kernel(
                 w3_w_raw[g][:].rearrange("p (m t) -> p m t", t=PACK),
             )
 
-        def deal_w4():
+        def deal_w4_words():
             for a in range(2):
                 deal(w4_w[:, a, :].bitcast(U16), w4_w_raw[:, a, :].bitcast(U16))
 
         def deal_w4_scales():
             deal(w4_s[:, :H], w4_s_raw[:])
-            for q in range(4):
-                nc.sync.dma_start(w4_s[32 * q : 32 * q + 4, H:].bitcast(I32), w4_s[32 * q + 4 : 32 * q + 8, :H].bitcast(I32))
+            for quad in range(QUADRANTS):
+                first = 32 * quad
+                nc.sync.dma_start(w4_s[first : first + 4, H:].bitcast(I32), w4_s[first + 4 : first + 8, :H].bitcast(I32))
 
         deal_w3_words(0)
         gather_words(0)
@@ -170,30 +181,29 @@ def tile_list_postal_digit_doubt_kernel(
         gated = {}
         h = {}
 
-        def gate(g, t, hf):
-            b = psum.tile([P, BANK], F32, name="work", bufs=6)
-            mx(b[:], q2[g], P * t, v[hf], True, True)
-            e = psum.tile([P, BANK], F32, name="work", bufs=6)
-            mx(e[:], (w3_w[:, BANK * g : BANK * (g + 1)], w3_s[4 * g :, :]), P * t, v[hf], True, True)
-            sig = ring.tile([P, BANK], F32, name="sig", bufs=3)
+        def gate(g, t, half):
+            b = psum.tile([P, BANK], F32, name="work", bufs=WORK_BANKS)
+            mx(b[:], q2[g], P * t, v[half], True, True)
+            e = psum.tile([P, BANK], F32, name="work", bufs=WORK_BANKS)
+            mx(e[:], (w3_w[:, BANK * g : BANK * (g + 1)], w3_s[4 * g :, :]), P * t, v[half], True, True)
+            sig = ring.tile([P, BANK], F32, name="sig", bufs=STREAM_BUFS)
             nc.scalar.activation(sig[:], b[:], ACT.Sigmoid)
-            prod = ring.tile([P, BANK], F32, name="prod", bufs=8)
-            nc.vector.tensor_tensor(prod[:], e[:], sig[:], ALU.mult)
-            gated[g, t, hf] = prod
+            gated[g, t, half] = ring.tile([P, BANK], F32, name="prod", bufs=GATED_BUFS)
+            nc.vector.tensor_tensor(gated[g, t, half][:], e[:], sig[:], ALU.mult)
 
-        def add(g, t, hf):
-            if hf == 0:
-                h[g, t] = ring.tile([P, S], F32, name="h", bufs=3)
-            a = psum.tile([P, BANK], F32, name="work", bufs=6)
-            mx(a[:], q1[g], P * t, v[hf], True, True)
-            dst, prod = h[g, t][:, BANK * hf : BANK * (hf + 1)], gated[g, t, hf]
-            first = POOL_COLS if hf == 0 else 0
-            if first:
+        def add(g, t, half):
+            if half == 0:
+                h[g, t] = ring.tile([P, S], F32, name="h", bufs=STREAM_BUFS)
+            a = psum.tile([P, BANK], F32, name="work", bufs=WORK_BANKS)
+            mx(a[:], q1[g], P * t, v[half], True, True)
+            dst, prod = h[g, t][:, BANK * half : BANK * (half + 1)], gated[g, t, half]
+            first = 0
+            if half == 0:
+                first = POOL_COLS
                 a_sb = ring.tile([P, POOL_COLS], F32, name="a_sb", bufs=2)
                 nc.scalar.copy(a_sb[:], a[:, :first])
                 nc.gpsimd.tensor_tensor(dst[:, :first], a_sb[:], prod[:, :first], ALU.add)
-            if first < BANK:
-                nc.vector.tensor_tensor(dst[:, first:], a[:, first:], prod[:, first:], ALU.add)
+            nc.vector.tensor_tensor(dst[:, first:], a[:, first:], prod[:, first:], ALU.add)
 
         def pick1(g, t):
             nc.vector.tensor_copy(x1[g][:, t, :], h[g, t][:].indirect(pos1_sb[:]))
@@ -202,16 +212,19 @@ def tile_list_postal_digit_doubt_kernel(
         x1q = []
         y = {}
 
-        def quantise_x1(g, split):
-            grouped = ring.tile([P, PACK * P1], BF16, name="grouped1", bufs=2, align_bytes=64)
-            dst, src = woven_views(grouped[:], x1[g])
-            if split > 0:
-                nc.vector.tensor_copy(dst[:, :split], src[:, :split])
-            nc.scalar.copy(dst[:, split:], src[:, split:])
-            codes, scales = quantise("x1q_%d" % g, grouped, P1)
+        def quantise_x1(g, runs_on_vector):
+            rounded = ring.tile([P, PACK * P1], BF16, name="grouped1", bufs=2, align_bytes=64)
+            dst, src = woven_views(rounded[:], x1[g])
+            if runs_on_vector > 0:
+                nc.vector.tensor_copy(dst[:, :runs_on_vector], src[:, :runs_on_vector])
+            nc.scalar.copy(dst[:, runs_on_vector:], src[:, runs_on_vector:])
+            codes, scales = quantise("x1q_%d" % g, rounded, P1)
             x1q.append((codes[:], scales[:]))
 
-        def quantise_second_halves():
+        def quantise_w1_first_group():
+            q1.extend(quantise_weights("q1_0", [raw1[0]], dealt_views))
+
+        def quantise_second_groups():
             both = quantise_weights("q21_1", [raw2[1], raw1[1]], dealt_views)
             q2.append(both[0])
             q1.append(both[1])
@@ -221,10 +234,10 @@ def tile_list_postal_digit_doubt_kernel(
 
         def y_passes(g, t, a):
             if a == 0:
-                if PACK * g + t >= 2:
-                    y[g, t] = psum.tile([P, P1], F32, name="work", bufs=6)
+                if PACK * g + t >= EARLY_BANKS:
+                    y[g, t] = psum.tile([P, P1], F32, name="work", bufs=WORK_BANKS)
                 else:
-                    y[g, t] = psum.tile([P, P1], F32, name="y", bufs=2)
+                    y[g, t] = psum.tile([P, P1], F32, name="y", bufs=EARLY_BANKS)
             col = BANK * g + P * t
             nc.tensor.matmul_mx(
                 out=y[g, t][:],
@@ -237,31 +250,31 @@ def tile_list_postal_digit_doubt_kernel(
             )
             mx(y[g, t][:], q5[g][a], P * t, x1q[a], False, a == 1)
 
-        units = [(g, t, hf) for g in range(2) for t in range(PACK) for hf in range(2)]
-        extras = {
-            0: lambda: q1.extend(quantise_weights("q1_0", [raw1[0]], dealt_views)),
-            3: quantise_second_halves,
+        units = [(g, t, half) for g in range(2) for t in range(PACK) for half in range(2)]
+        side_jobs = {
+            0: quantise_w1_first_group,
+            3: quantise_second_groups,
             5: lambda: deal_w3_words(1),
-            6: deal_w4,
+            6: deal_w4_words,
             9: lambda: quantise_w5(0),
             10: deal_w4_scales,
             11: lambda: quantise_x1(0, 0),
             13: lambda: quantise_w5(1),
         }
-        LAG = 1
-        for i in range(len(units) + LAG + 1):
-            if i < len(units):
-                gate(*units[i])
-            if LAG <= i < len(units) + LAG:
-                add(*units[i - LAG])
-            if i > LAG and units[i - LAG - 1][2] == 1:
-                pick1(*units[i - LAG - 1][:2])
-            if i in extras:
-                extras[i]()
+        for turn in range(len(units) + 2):
+            if turn < len(units):
+                gate(*units[turn])
+            if 1 <= turn <= len(units):
+                add(*units[turn - 1])
+            if turn >= 2 and units[turn - 2][2] == 1:
+                pick1(*units[turn - 2][:2])
+            if turn in side_jobs:
+                side_jobs[turn]()
+
         tiles = [(g, t) for g in range(2) for t in range(PACK)]
         for g, t in tiles:
             y_passes(g, t, 0)
-        quantise_x1(1, WEAVE_SPLIT)
+        quantise_x1(1, X1_RUNS_ON_VECTOR)
         q6 = quantise_weights("q6", raw6, woven_views)
 
         x2 = {}
@@ -269,38 +282,38 @@ def tile_list_postal_digit_doubt_kernel(
 
         def step(g, t):
             y_passes(g, t, 1)
-            sig = ring.tile([P, P1], F32, name="sig", bufs=3)
+            sig = ring.tile([P, P1], F32, name="sig", bufs=STREAM_BUFS)
             nc.scalar.activation(sig[:], y[g, t][:], ACT.Sigmoid, scale=2.0)
-            x2[g, t] = ring.tile([P, P1], F32, name="x2", bufs=3)
-            nc.vector.scalar_tensor_tensor(x2[g, t][:], sig[:], 1.0 / 18.0, x1[g][:, t, :], ALU.add, ALU.mult)
+            x2[g, t] = ring.tile([P, P1], F32, name="x2", bufs=STREAM_BUFS)
+            nc.vector.scalar_tensor_tensor(x2[g, t][:], sig[:], STEP_SHIFT, x1[g][:, t, :], ALU.add, ALU.mult)
 
         def pick2(g, t):
             nc.vector.tensor_copy(x3[g][:, t, :], x2[g, t][:].indirect(pos2_sb[:]))
 
-        def last_passes(g, split):
-            grouped = ring.tile([P, PACK * P2], BF16, name="x3_bf", bufs=2, align_bytes=64)
-            dst, src = woven_views(grouped[:], x3[g])
-            if split > 0:
-                nc.vector.tensor_scalar(dst[:, :split], src[:, :split], 1.8, None, ALU.mult)
-            nc.scalar.activation(dst[:, split:], src[:, split:], ACT.Copy, scale=1.8)
-            codes, scales = quantise("x3q_%d" % g, grouped, P2)
+        def last_passes(g, runs_on_vector):
+            rounded = ring.tile([P, PACK * P2], BF16, name="x3_bf", bufs=2, align_bytes=64)
+            dst, src = woven_views(rounded[:], x3[g])
+            if runs_on_vector > 0:
+                nc.vector.tensor_scalar(dst[:, :runs_on_vector], src[:, :runs_on_vector], STEP_GAIN, None, ALU.mult)
+            nc.scalar.activation(dst[:, runs_on_vector:], src[:, runs_on_vector:], ACT.Copy, scale=STEP_GAIN)
+            codes, scales = quantise("x3q_%d" % g, rounded, P2)
             for u in range(N // P):
                 if g == 0:
-                    o.append(psum.tile([P, P2], F32, name="work", bufs=6))
+                    o.append(psum.tile([P, P2], F32, name="work", bufs=WORK_BANKS))
                 mx(o[u][:], q6[g], P * u, (codes[:], scales[:]), g == 0, g == 1)
 
-        for i in range(len(tiles) + 1):
-            if i < len(tiles):
-                step(*tiles[i])
-            if i >= 1:
-                pick2(*tiles[i - 1])
-            if i == PACK + 1:
+        for turn in range(len(tiles) + 1):
+            if turn < len(tiles):
+                step(*tiles[turn])
+            if turn >= 1:
+                pick2(*tiles[turn - 1])
+            if turn == PACK + 1:
                 last_passes(0, 0)
-        last_passes(1, WEAVE3_SPLIT)
+        last_passes(1, X3_RUNS_ON_VECTOR)
 
         for u in range(N // P):
-            sig = ring.tile([P, P2], F32, name="sig_out", bufs=4)
+            sig = ring.tile([P, P2], F32, name="sig_out", bufs=N // P)
             nc.scalar.activation(sig[:], o[u][:], ACT.Sigmoid)
-            res = ring.tile([P, P2], F32, name="res", bufs=4)
+            res = ring.tile([P, P2], F32, name="res", bufs=N // P)
             nc.vector.tensor_tensor(res[:], sig[:], sig[:], ALU.mult)
             nc.sync.dma_start(out[P * u : P * (u + 1), :], res[:])

from contextlib import ExitStack

import concourse.mybir as mybir

F32 = mybir.dt.float32
BF16 = mybir.dt.bfloat16
I32 = mybir.dt.int32
U32 = mybir.dt.uint32
U16 = mybir.dt.uint16
U8 = mybir.dt.uint8
FP8X4 = mybir.dt.float8_e4m3fn_x4
FP4X4 = mybir.dt.float4_e2m1fn_x4
ACT = mybir.ActivationFunctionType
ALU = mybir.AluOpType

K, H, N, T, S, P1, P2 = 512, 1024, 512, 4096, 1024, 512, 256
FLOPS = 2 * (3 * K * H * S + 2 * H * H * P1 + H * N * P2)

P = 128
PACK = 4
PASS = P * PACK
BANK = 512
QUADRANTS = 4
STEP_GAIN = 1.8
STEP_SHIFT = 1.0 / 18.0

POOL_COLS = 384
X1_RUNS_ON_VECTOR = 88
X3_RUNS_ON_VECTOR = 44

RAW_BUFS = 6
GATED_BUFS = 8
STREAM_BUFS = 3
WORK_BANKS = 6
EARLY_BANKS = 2


def tile_list_postal_digit_doubt_kernel(
    tc, tab_words, tab_scales, offs, pos1, pos2, w1, w2, w3_words, w3_scales, w4_words, w4_scales, w5, w6, out
):
    nc = tc.nc
    with ExitStack() as ctx:
        keep = ctx.enter_context(tc.tile_pool(name="keep", bufs=1))
        ring = ctx.enter_context(tc.tile_pool(name="ring", bufs=2))
        psum = ctx.enter_context(tc.psum_pool(name="psum", bufs=1))

        def held(name, shape, dtype):
            return keep.tile(shape, dtype, name=name, align_bytes=64)

        tab_s = held("tab_s", [P, T], U8)
        w3_s_raw = held("w3_s_raw", [P, BANK], U8)
        w4_s_raw = held("w4_s_raw", [P, H], U8)
        w4_s = held("w4_s", [P, 2 * H], U8)
        nc.vector.memset(tab_s[:].bitcast(I32), 0)
        nc.vector.memset(w3_s_raw[:].bitcast(I32), 0)
        nc.vector.memset(w4_s_raw[:].bitcast(I32), 0)
        nc.vector.memset(w4_s[:, H:].bitcast(I32), 0)

        offs_sb = keep.tile([P, S // 16], U16, name="offs_sb")
        pos1_sb = keep.tile([P, P1 // 16], U16, name="pos1_sb")
        pos2_sb = keep.tile([P, P2 // 16], U16, name="pos2_sb")
        tab_w = held("tab_w", [P, T], I32)
        w3_w_raw = [held("w3_w_raw%d" % g, [P, BANK], I32) for g in range(2)]
        w4_w_raw = held("w4_w_raw", [P, 2, H // 2], I32)
        w3_dram = w3_words[0].rearrange("p c i -> p (c i)").bitcast(I32)

        def load_rows(w, a, g):
            raw = ring.tile([P, PACK, BANK], F32, name="raw", bufs=RAW_BUFS)
            piece = w[PASS * a : PASS * (a + 1), BANK * g : BANK * (g + 1)]
            nc.sync.dma_start(raw[:], piece.rearrange("(p j) c -> p j c", j=PACK))
            return raw

        def load_scale_rows(tile, row_sets):
            for quad in range(QUADRANTS):
                nc.sync.dma_start(
                    tile[32 * quad : 32 * quad + 4 * row_sets.shape[0], :].bitcast(I32),
                    row_sets[:, 4 * quad : 4 * quad + 4, :].bitcast(I32),
                )

        raw1, raw2, raw5 = {}, {}, {}
        nc.sync.dma_start(offs_sb[:], offs)
        raw2[0] = load_rows(w2, 0, 0)
        nc.sync.dma_start(w3_w_raw[0][:], w3_dram[:, :BANK])
        load_scale_rows(tab_s, tab_scales)
        nc.sync.dma_start(tab_w[:], tab_words[0].rearrange("p c i -> p (c i)").bitcast(I32))
        load_scale_rows(w3_s_raw, w3_scales[0].rearrange("q (g c) -> g q c", g=2))
        raw1[0] = load_rows(w1, 0, 0)
        nc.sync.dma_start(pos1_sb[:], pos1)
        nc.sync.dma_start(w4_w_raw[:], w4_words.bitcast(I32).rearrange("a p c -> p a c"))
        raw2[1] = load_rows(w2, 0, 1)
        nc.sync.dma_start(w3_w_raw[1][:], w3_dram[:, BANK:])
        raw1[1] = load_rows(w1, 0, 1)
        for g in range(2):
            for a in range(2):
                raw5[a, g] = load_rows(w5, a, g)
        nc.sync.dma_start(pos2_sb[:], pos2)
        load_scale_rows(w4_s_raw, w4_scales)
        raw6 = [load_rows(w6, a, 0) for a in range(2)]

        def dealt_views(rounded, raw):
            dst = rounded.rearrange("p (t n i j) -> p n j i t", t=PACK, i=2, j=PACK)
            src = raw[:].rearrange("p j (n i t) -> p n j i t", i=2, t=PACK)
            return dst, src

        def woven_views(rounded, rows):
            dst = rounded.rearrange("p (c i t) -> p c t i", i=4, t=PACK)
            src = rows[:].rearrange("p t (c i) -> p c t i", i=4)
            return dst, src

        def quantise(name, rounded, width):
            codes = held(name + "_codes", [P, width], U32)
            scales = held(name + "_scales", [P, width], U8)
            nc.vector.quantize_mx(out=codes[:].bitcast(FP8X4), scales=scales[:], in_=rounded[:])
            return codes, scales

        def quantise_weights(name, raws, views):
            width = PACK * BANK
            rounded = ring.tile([P, width * len(raws)], BF16, name="grouped%d" % len(raws), bufs=2, align_bytes=64)
            for i, raw in enumerate(raws):
                dst, src = views(rounded[:, width * i : width * (i + 1)], raw)
                for part in range(2):
                    runs = slice(dst.shape[1] // 2 * part, dst.shape[1] // 2 * (part + 1))
                    nc.scalar.copy(dst[:, runs], src[:, runs])
            codes, scales = quantise(name, rounded, BANK * len(raws))
            return [(codes[:, BANK * i : BANK * (i + 1)], scales[:, BANK * i : BANK * (i + 1)]) for i in range(len(raws))]

        def mx(acc, lhs, col, rhs, start, stop):
            nc.tensor.matmul_mx(
                out=acc,
                lhsT=lhs[0][:, col : col + P].bitcast(FP8X4),
                lhsT_scale=lhs[1][:, col : col + P],
                rhs=rhs[0].bitcast(FP8X4),
                rhs_scale=rhs[1],
                start=start,
                stop=stop,
            )

        v_s = held("v_s", [P, S], U8)
        nc.vector.tensor_copy(v_s[:], tab_s[:].indirect(offs_sb[:]))
        q2 = quantise_weights("q2_0", [raw2[0]], dealt_views)
        w3_w = held("w3_w", [P, H], I32)
        w3_s = held("w3_s", [P, BANK], U8)
        w4_w = held("w4_w", [P, 2, 2 * H], U8)
        v = []

        def gather_words(half):
            words = held("v_w%d" % half, [P, BANK], U32)
            cols = BANK // 16
            nc.vector.tensor_copy(words[:], tab_w[:].bitcast(U32).indirect(offs_sb[:, cols * half : cols * (half + 1)]))
            v.append((words[:], v_s[:, BANK * half : BANK * (half + 1)]))

        def deal(dst, src):
            nc.vector.tensor_copy(
                dst.rearrange("p (g t m) -> p g t m", t=PACK, m=P), src.rearrange("p (g m t) -> p g t m", t=PACK, m=P)
            )

        def deal_w3_words(g):
            nc.vector.tensor_copy(
                w3_w[:, BANK * g : BANK * (g + 1)].rearrange("p (t m) -> p m t", t=PACK),
                w3_w_raw[g][:].rearrange("p (m t) -> p m t", t=PACK),
            )

        def deal_w4_words():
            for a in range(2):
                deal(w4_w[:, a, :].bitcast(U16), w4_w_raw[:, a, :].bitcast(U16))

        def deal_w4_scales():
            deal(w4_s[:, :H], w4_s_raw[:])
            for quad in range(QUADRANTS):
                first = 32 * quad
                nc.sync.dma_start(w4_s[first : first + 4, H:].bitcast(I32), w4_s[first + 4 : first + 8, :H].bitcast(I32))

        deal_w3_words(0)
        gather_words(0)
        deal(w3_s[:], w3_s_raw[:])
        gather_words(1)
        q1 = []

        x1 = [held("x1_%d" % g, [P, PACK, P1], F32) for g in range(2)]
        x3 = [held("x3_%d" % g, [P, PACK, P2], F32) for g in range(2)]
        gated = {}
        h = {}

        def gate(g, t, half):
            b = psum.tile([P, BANK], F32, name="work", bufs=WORK_BANKS)
            mx(b[:], q2[g], P * t, v[half], True, True)
            e = psum.tile([P, BANK], F32, name="work", bufs=WORK_BANKS)
            mx(e[:], (w3_w[:, BANK * g : BANK * (g + 1)], w3_s[4 * g :, :]), P * t, v[half], True, True)
            sig = ring.tile([P, BANK], F32, name="sig", bufs=STREAM_BUFS)
            nc.scalar.activation(sig[:], b[:], ACT.Sigmoid)
            gated[g, t, half] = ring.tile([P, BANK], F32, name="prod", bufs=GATED_BUFS)
            nc.vector.tensor_tensor(gated[g, t, half][:], e[:], sig[:], ALU.mult)

        def add(g, t, half):
            if half == 0:
                h[g, t] = ring.tile([P, S], F32, name="h", bufs=STREAM_BUFS)
            a = psum.tile([P, BANK], F32, name="work", bufs=WORK_BANKS)
            mx(a[:], q1[g], P * t, v[half], True, True)
            dst, prod = h[g, t][:, BANK * half : BANK * (half + 1)], gated[g, t, half]
            first = 0
            if half == 0:
                first = POOL_COLS
                a_sb = ring.tile([P, POOL_COLS], F32, name="a_sb", bufs=2)
                nc.scalar.copy(a_sb[:], a[:, :first])
                nc.gpsimd.tensor_tensor(dst[:, :first], a_sb[:], prod[:, :first], ALU.add)
            nc.vector.tensor_tensor(dst[:, first:], a[:, first:], prod[:, first:], ALU.add)

        def pick1(g, t):
            nc.vector.tensor_copy(x1[g][:, t, :], h[g, t][:].indirect(pos1_sb[:]))

        q5 = {}
        x1q = []
        y = {}

        def quantise_x1(g, runs_on_vector):
            rounded = ring.tile([P, PACK * P1], BF16, name="grouped1", bufs=2, align_bytes=64)
            dst, src = woven_views(rounded[:], x1[g])
            if runs_on_vector > 0:
                nc.vector.tensor_copy(dst[:, :runs_on_vector], src[:, :runs_on_vector])
            nc.scalar.copy(dst[:, runs_on_vector:], src[:, runs_on_vector:])
            codes, scales = quantise("x1q_%d" % g, rounded, P1)
            x1q.append((codes[:], scales[:]))

        def quantise_w1_first_group():
            q1.extend(quantise_weights("q1_0", [raw1[0]], dealt_views))

        def quantise_second_groups():
            both = quantise_weights("q21_1", [raw2[1], raw1[1]], dealt_views)
            q2.append(both[0])
            q1.append(both[1])

        def quantise_w5(g):
            q5[g] = quantise_weights("q5_%d" % g, [raw5[0, g], raw5[1, g]], dealt_views)

        def y_passes(g, t, a):
            if a == 0:
                if PACK * g + t >= EARLY_BANKS:
                    y[g, t] = psum.tile([P, P1], F32, name="work", bufs=WORK_BANKS)
                else:
                    y[g, t] = psum.tile([P, P1], F32, name="y", bufs=EARLY_BANKS)
            col = BANK * g + P * t
            nc.tensor.matmul_mx(
                out=y[g, t][:],
                lhsT=w4_w[:, a, 2 * col : 2 * (col + P)].bitcast(FP4X4),
                lhsT_scale=w4_s[:, H * a + col : H * a + col + P],
                rhs=x1q[a][0].bitcast(FP8X4),
                rhs_scale=x1q[a][1],
                start=(a == 0),
                stop=False,
            )
            mx(y[g, t][:], q5[g][a], P * t, x1q[a], False, a == 1)

        units = [(g, t, half) for g in range(2) for t in range(PACK) for half in range(2)]
        side_jobs = {
            0: quantise_w1_first_group,
            3: quantise_second_groups,
            5: lambda: deal_w3_words(1),
            6: deal_w4_words,
            9: lambda: quantise_w5(0),
            10: deal_w4_scales,
            11: lambda: quantise_x1(0, 0),
            13: lambda: quantise_w5(1),
        }
        for turn in range(len(units) + 2):
            if turn < len(units):
                gate(*units[turn])
            if 1 <= turn <= len(units):
                add(*units[turn - 1])
            if turn >= 2 and units[turn - 2][2] == 1:
                pick1(*units[turn - 2][:2])
            if turn in side_jobs:
                side_jobs[turn]()

        tiles = [(g, t) for g in range(2) for t in range(PACK)]
        for g, t in tiles:
            y_passes(g, t, 0)
        quantise_x1(1, X1_RUNS_ON_VECTOR)
        q6 = quantise_weights("q6", raw6, woven_views)

        x2 = {}
        o = []

        def step(g, t):
            y_passes(g, t, 1)
            sig = ring.tile([P, P1], F32, name="sig", bufs=STREAM_BUFS)
            nc.scalar.activation(sig[:], y[g, t][:], ACT.Sigmoid, scale=2.0)
            x2[g, t] = ring.tile([P, P1], F32, name="x2", bufs=STREAM_BUFS)
            nc.vector.scalar_tensor_tensor(x2[g, t][:], sig[:], STEP_SHIFT, x1[g][:, t, :], ALU.add, ALU.mult)

        def pick2(g, t):
            nc.vector.tensor_copy(x3[g][:, t, :], x2[g, t][:].indirect(pos2_sb[:]))

        def last_passes(g, runs_on_vector):
            rounded = ring.tile([P, PACK * P2], BF16, name="x3_bf", bufs=2, align_bytes=64)
            dst, src = woven_views(rounded[:], x3[g])
            if runs_on_vector > 0:
                nc.vector.tensor_scalar(dst[:, :runs_on_vector], src[:, :runs_on_vector], STEP_GAIN, None, ALU.mult)
            nc.scalar.activation(dst[:, runs_on_vector:], src[:, runs_on_vector:], ACT.Copy, scale=STEP_GAIN)
            codes, scales = quantise("x3q_%d" % g, rounded, P2)
            for u in range(N // P):
                if g == 0:
                    o.append(psum.tile([P, P2], F32, name="work", bufs=WORK_BANKS))
                mx(o[u][:], q6[g], P * u, (codes[:], scales[:]), g == 0, g == 1)

        for turn in range(len(tiles) + 1):
            if turn < len(tiles):
                step(*tiles[turn])
            if turn >= 1:
                pick2(*tiles[turn - 1])
            if turn == PACK + 1:
                last_passes(0, 0)
        last_passes(1, X3_RUNS_ON_VECTOR)

        for u in range(N // P):
            sig = ring.tile([P, P2], F32, name="sig_out", bufs=N // P)
            nc.scalar.activation(sig[:], o[u][:], ACT.Sigmoid)
            res = ring.tile([P, P2], F32, name="res", bufs=N // P)
            nc.vector.tensor_tensor(res[:], sig[:], sig[:], ALU.mult)
            nc.sync.dma_start(out[P * u : P * (u + 1), :], res[:])
